import numpy as np
import ml_dtypes


def mxq(x, axis, fmt="e4m3"):
    dtype, down = {"e4m3": (ml_dtypes.float8_e4m3fn, 7), "e5m2": (ml_dtypes.float8_e5m2, 14)}[fmt]
    v = np.moveaxis(np.asarray(x, np.float32).astype(ml_dtypes.bfloat16).astype(np.float64), axis, -1)
    blocks = v.reshape(v.shape[:-1] + (-1, 32))
    amax = np.abs(blocks).max(-1, keepdims=True)
    byte = np.maximum(np.where(amax > 0, np.frexp(amax)[1] - 1 + 127, 0) - down, 1)
    scale = np.exp2(byte - 127.0)
    codes = (blocks / scale).astype(np.float32).astype(dtype).astype(np.float64)
    return np.moveaxis((codes * scale).reshape(v.shape), -1, axis)


WIDE = False


def mx_kscale(k):
    if not WIDE:
        return np.ones(k)
    levels = np.array([10, -10, 5, -5, 0])
    if k % 512:
        return np.exp2(np.random.permutation(np.resize(levels, k // 32))).repeat(32)
    a = np.empty((k // 512, 16))
    for p in range(k // 512):
        a[p, :8] = np.random.permutation(np.resize(levels, 8))
        for g in range(8):
            far = levels[np.abs(levels - a[p, g]) >= 10]
            a[p, g + 8] = far[np.random.randint(len(far))]
    return np.exp2(a.ravel()).repeat(32)


def f64(x):
    return np.asarray(x).astype(np.float64)


def striped(idx):
    return np.tile(idx.reshape(-1, 16).T, (8, 1)).astype(np.uint16)


def unstriped(offs):
    return offs[:16].T.reshape(-1).astype(np.int64)


def striped8(idx):
    return np.concatenate([x.reshape(-1, 16).T for x in idx]).astype(np.uint16)


def runs(offs, k):
    lists = np.stack([offs[16 * r : 16 * r + 16].T.reshape(-1) for r in range(8)]).astype(np.int64)
    return lists[np.arange(k) % 512 // 64]


def pack_weight(w):
    k, n = w.shape
    w = f64(np.asarray(w, np.float32).astype(ml_dtypes.bfloat16)).reshape(k // 32, 32, n)
    amax = np.abs(w).max(1)
    byte = np.clip(np.where(amax > 0, np.frexp(amax)[1] - 1 + 127 - 7, 1), 1, 254)
    scaled = (w * np.exp2(127.0 - byte)[:, None, :]).reshape(k, n).astype(np.float32)
    words = np.ascontiguousarray(scaled.reshape(k // 512, 128, 4, n).transpose(0, 1, 3, 2)).astype(ml_dtypes.float8_e4m3fn).view(np.uint8)
    return words, np.ascontiguousarray(byte.astype(np.uint8).reshape(k // 512, 16, n))


def unpack_weight(words, scales):
    g, p, n, _ = words.shape
    vals = np.ascontiguousarray(words).view(ml_dtypes.float8_e4m3fn).astype(np.float64) * np.repeat(np.exp2(scales.astype(np.float64) - 127.0), 8, axis=1)[..., None]
    return vals.transpose(0, 1, 3, 2).reshape(g * 512, n)

def planes(y):
    n, m = y.shape
    v = y.astype(np.float32).astype(ml_dtypes.bfloat16).astype(np.float64).reshape(n // 32, 32, m)
    top = np.abs(v).max(1)
    byte = np.clip(np.where(top > 0, np.frexp(top)[1] - 1 + 127 - 7, 1), 1, 254)
    codes = (v * np.exp2(127.0 - byte)[:, None, :]).reshape(n, m).astype(np.float32).astype(ml_dtypes.float8_e4m3fn).view(np.uint8)
    words = codes.reshape(n // 512, 128, 4, m).transpose(0, 1, 3, 2)
    return np.ascontiguousarray(words), np.ascontiguousarray(byte.astype(np.uint8).reshape(n // 512, 16, m))


K, T, S, N, H, W, U = 512, 2048, 512, 512, 512, 256, 1024


def setup_inputs():
    n = np.random.standard_normal
    s = mx_kscale(K)[:, None]
    u = mx_kscale(H)
    packed_xT = pack_weight(n((K, T)) * s)
    packed_w1 = pack_weight(n((K, H)) / np.sqrt(K) / s)
    packed_w2 = pack_weight(n((K, H)) / np.sqrt(K) / s)
    packed_w3 = pack_weight(n((H, N)) / np.sqrt(H) / u[:, None])
    return {
        "x_words": packed_xT[0],
        "x_scales": packed_xT[1],
        "w1_words": packed_w1[0],
        "w1_scales": packed_w1[1],
        "w2_words": packed_w2[0],
        "w2_scales": packed_w2[1],
        "gn": (np.random.uniform(0.5, 1.5, (H, 1)) * u[:, None]).astype(np.float32),
        "w3_words": packed_w3[0],
        "w3_scales": packed_w3[1],
        "mem": n((N, U)).astype(np.float32),
        "offs": striped(np.random.permutation(T)[:S]),
        "two": striped(np.random.permutation(T)[:S]),
        "n1": striped8(np.stack([np.random.permutation(S)[:W] for _ in range(8)])),
        "n2": striped8(np.stack([np.random.permutation(S)[:W] for _ in range(8)])),
        "n3": striped8(np.stack([np.random.permutation(U)[:S] for _ in range(8)])),
        "n4": striped8(np.stack([np.random.permutation(U) for _ in range(8)])),
    }


def reference(x_words, x_scales, w1_words, w1_scales, w2_words, w2_scales, gn, w3_words, w3_scales, mem, offs, two, n1, n2, n3, n4):
    x_two = unpack_weight(x_words, x_scales)[:, unstriped(two)]
    d = unpack_weight(w2_words, w2_scales).T @ x_two
    xq = unpack_weight(x_words, x_scales)[:, unstriped(offs)]
    y = unpack_weight(w1_words, w1_scales).T @ xq
    ra = d[np.arange(H)[:, None], runs(n2, H)] - (0.5 * (y[np.arange(H)[:, None], runs(n1, H)]))
    ds = y.copy()
    ds[np.arange(H)[:, None], runs(n1, H)] = ra
    z = f64(gn) * ds
    h = unpack_weight(w3_words, w3_scales).T @ mxq(z, 0, "e4m3")
    pg = f64(mem).copy()
    pg[np.arange(N)[:, None], runs(n3, N)] = h
    out_0 = pg - (0.5 * (pg[np.arange(N)[:, None], runs(n4, N)]))
    return (out_0,) + planes(out_0)

@@ -1,0 +1,193 @@
+from contextlib import ExitStack
+
+import concourse.mybir as mybir
+
+K, T, S, N, H, W, U = 512, 2048, 512, 512, 512, 256, 1024
+FLOPS = 2 * K * H * S * 2 + 2 * H * N * S
+
+F32 = mybir.dt.float32
+BF16 = mybir.dt.bfloat16
+I32 = mybir.dt.int32
+U32 = mybir.dt.uint32
+U16 = mybir.dt.uint16
+U8 = mybir.dt.uint8
+FP8X4 = mybir.dt.float8_e4m3fn_x4
+MULT = mybir.AluOpType.mult
+ADD = mybir.AluOpType.add
+COPY = mybir.ActivationFunctionType.Copy
+
+P = 128
+PACK = 4
+QUADRANTS = 4
+GROUP = 16
+
+
+def words_view(words):
+    return words[0].rearrange("p n t -> p (n t)").bitcast(I32)
+
+
+def load_scale_rows(nc, plane, scales, first):
+    for q in range(QUADRANTS):
+        nc.sync.dma_start(out=plane[32 * q + first : 32 * q + first + 4, :].bitcast(I32), in_=scales[0, 4 * q : 4 * q + 4, :].bitcast(I32))
+
+
+def deal(nc, dealt, raw):
+    nc.vector.tensor_copy(out=dealt[:].rearrange("p (t m) -> p m t", t=PACK), in_=raw[:].rearrange("p (m t) -> p m t", t=PACK))
+
+
+def tile_picked_twlputbpagem_none_po_kernel(tc, x_words, x_scales, w1_words, w1_scales, w2_words, w2_scales, gn, w3_words, w3_scales, mem, offs, two, n1, n2, n3, n4, out_0, out_1, out_2):
+    nc = tc.nc
+    with ExitStack() as ctx:
+        keep = ctx.enter_context(tc.tile_pool(name="keep", bufs=1))
+        psum = ctx.enter_context(tc.psum_pool(name="psum", bufs=1))
+
+        def load_list(src, name):
+            dst = keep.tile(list(src.shape), U16, name=name)
+            nc.sync.dma_start(dst[:], src)
+            return dst
+
+        x_plane = keep.tile([P, T], U8, align_bytes=64, tag="page3")
+        w12_plane = keep.tile([P, H], U8, align_bytes=64, tag="w_plane")
+        nc.gpsimd.memset(x_plane[:].bitcast(I32), 0)
+        nc.vector.memset(w12_plane[:].bitcast(I32), 0)
+
+        offs_t = load_list(offs, "offs_t")
+        load_scale_rows(nc, x_plane, x_scales, 0)
+        two_t = load_list(two, "two_t")
+        x_codes = keep.tile([P, T], U32, align_bytes=64, tag="page0")
+        nc.sync.dma_start(out=x_codes[:].bitcast(I32), in_=words_view(x_words))
+        w1_raw = keep.tile([P, H], U32, align_bytes=64, tag="w_raw")
+        nc.sync.dma_start(out=w1_raw[:].bitcast(I32), in_=words_view(w1_words))
+        load_scale_rows(nc, w12_plane, w1_scales, 0)
+        load_scale_rows(nc, w12_plane, w2_scales, 4)
+        w2_raw = keep.tile([P, H], U32, align_bytes=64, tag="page1")
+        nc.sync.dma_start(out=w2_raw[:].bitcast(I32), in_=words_view(w2_words))
+        n1_t = load_list(n1, "n1_t")
+        n2_t = load_list(n2, "n2_t")
+        gain = keep.tile([P, PACK], F32)
+        nc.sync.dma_start(out=gain[:], in_=gn.rearrange("(p t) o -> p (t o)", t=PACK))
+        n3_t = load_list(n3, "n3_t")
+        n4_t = load_list(n4, "n4_t")
+
+        xy_scales = keep.tile([P, S], U8, align_bytes=64)
+        xd_scales = keep.tile([P, S], U8, align_bytes=64, tag="page2")
+        xy_codes = keep.tile([P, S], U32, align_bytes=64)
+        xd_codes = keep.tile([P, S], U32, align_bytes=64)
+        w1_codes = keep.tile([P, H], U32, align_bytes=64)
+        w2_codes = keep.tile([P, H], U32, align_bytes=64)
+        w12_scales = keep.tile([P, H], U8, align_bytes=64)
+        nc.vector.tensor_copy(xy_scales[:], x_plane[:].indirect(offs_t[:]))
+        nc.vector.tensor_copy(xd_scales[:], x_plane[:].indirect(two_t[:]))
+        nc.vector.tensor_copy(xy_codes[:], x_codes[:].indirect(offs_t[:]))
+        deal(nc, w1_codes, w1_raw)
+        deal(nc, w12_scales, w12_plane)
+        deal(nc, w2_codes, w2_raw)
+        nc.vector.tensor_copy(xd_codes[:], x_codes[:].indirect(two_t[:]))
+
+        def product(bank, width, w_codes, w_scales, t, codes, scales, at=0):
+            cols = slice(P * t, P * (t + 1))
+            nc.tensor.matmul_mx(out=bank[:, at : at + width], lhsT=w_codes[:, cols].bitcast(FP8X4), lhsT_scale=w_scales[:, cols],
+                                rhs=codes.bitcast(FP8X4), rhs_scale=scales, start=True, stop=True)
+
+        ys = [keep.tile([P, S], F32, name=f"y{t}") for t in range(PACK)]
+        dd = [keep.tile([P, S], F32, name=f"d{t}") for t in range(PACK)]
+        for t in range(PACK):
+            bank = psum.tile([P, S], F32, tag=f"bank{t}", name=f"ybank{t}")
+            product(bank, S, w1_codes, w12_scales[:], t, xy_codes[:], xy_scales[:])
+            nc.scalar.activation(ys[t][:], bank[:], COPY)
+        for t in range(PACK):
+            bank = psum.tile([P, S], F32, tag=f"bank{PACK + t}", name=f"dbank{t}")
+            product(bank, S, w2_codes, w12_scales[4:P, :], t, xd_codes[:], xd_scales[:])
+            nc.scalar.activation(dd[t][:], bank[:], COPY)
+
+        w3_raw = keep.tile([P, N], U32, align_bytes=64, tag="w_raw")
+        nc.sync.dma_start(out=w3_raw[:].bitcast(I32), in_=words_view(w3_words))
+        w3_plane = keep.tile([P, N], U8, align_bytes=64, tag="w_plane")
+        nc.gpsimd.memset(w3_plane[:].bitcast(I32), 0)
+        load_scale_rows(nc, w3_plane, w3_scales, 0)
+        mem_rows = mem.rearrange("(p t) w -> p t w", t=PACK)
+        pg = [keep.tile([P, U], F32, name=f"pg{t}", tag=f"page{t}", align_bytes=64) for t in range(PACK)]
+        for t in range(PACK):
+            nc.sync.dma_start(out=pg[t][:], in_=mem_rows[:, t, :])
+
+        half_y = [keep.tile([P, W], F32, name=f"half_y{t}") for t in range(PACK - 1)]
+        half_y.append(keep.tile([P, W], F32, name="half_y3", tag="late_words", align_bytes=64))
+        picked_d = [keep.tile([P, W], F32, name=f"picked_d{t}") for t in range(PACK - 1)]
+        picked_d.append(keep.tile([P, W], F32, name="picked_d3", tag="late_bytes", align_bytes=64))
+        for t in range(PACK):
+            nc.vector.tensor_scalar(half_y[t][:], ys[t][:].indirect(n1_t[:]), -0.5, 0.0, MULT, ADD)
+        z = keep.tile([P, S, PACK], BF16, align_bytes=64)
+        z_chunks = [(0, 128), (128, 256), (256, 512)]
+        for t in range(PACK):
+            nc.vector.tensor_copy(picked_d[t][:], dd[t][:].indirect(n2_t[:]))
+            nc.vector.tensor_tensor(ys[t][:].indirect(n1_t[:]), picked_d[t][:], half_y[t][:], ADD)
+            if t < PACK - 1:
+                nc.scalar.activation(z[:, :, t], ys[t][:], COPY, scale=gain[:, t : t + 1])
+
+        w3_codes = keep.tile([P, N], U32, tag="late_words", align_bytes=64)
+        w3_dealt = keep.tile([P, N], U8, tag="late_bytes", align_bytes=64)
+        deal(nc, w3_codes, w3_raw)
+        deal(nc, w3_dealt, w3_plane)
+
+        z_codes = keep.tile([P, S], U32, align_bytes=64)
+        z_scales = keep.tile([P, S], U8, align_bytes=64)
+        hs = [keep.tile([P, S], F32, name=f"h{t}") for t in range(PACK)]
+
+        def quantize_z(a, b):
+            t = PACK - 1
+            nc.scalar.activation(z[:, a:b, t], ys[t][:, a:b], COPY, scale=gain[:, t : t + 1])
+            nc.vector.quantize_mx(out=z_codes[:, a:b].bitcast(FP8X4), scales=z_scales[:, a:b], in_=z[:, a:b, :].rearrange("p s t -> p (s t)"))
+
+        def scatter_h(t, a, b):
+            nc.vector.tensor_copy(pg[t][:].indirect(n3_t[:, a // GROUP : b // GROUP]), hs[t][:, a:b])
+
+        a0, b0 = z_chunks[0]
+        quantize_z(a0, b0)
+        early = range(2)
+        for t in early:
+            bank = psum.tile([P, S], F32, tag=f"bank{t}", name=f"hbank_a{t}")
+            product(bank, b0, w3_codes, w3_dealt[:], t, z_codes[:, a0:b0], z_scales[:, a0:b0])
+            nc.scalar.activation(hs[t][:, a0:b0], bank[:, a0:b0], COPY)
+            scatter_h(t, a0, b0)
+        for a, b in z_chunks[1:]:
+            quantize_z(a, b)
+        minus_half = [keep.tile([P, U], F32, name=f"minus_half{t}") for t in range(PACK)]
+        for t in range(PACK):
+            bank = psum.tile([P, S], F32, tag=f"bank{PACK + t}", name=f"hbank_b{t}")
+            if t in early:
+                for a, b in z_chunks[1:]:
+                    product(bank, b - a, w3_codes, w3_dealt[:], t, z_codes[:, a:b], z_scales[:, a:b], at=a)
+                first = b0
+            else:
+                product(bank, S, w3_codes, w3_dealt[:], t, z_codes[:], z_scales[:])
+                first = 0
+            nc.scalar.activation(hs[t][:, first:S], bank[:, first:S], COPY)
+            scatter_h(t, first, S)
+            nc.scalar.activation(minus_half[t][:], pg[t][:], COPY, scale=-0.5)
+
+        out_rows = out_0.rearrange("(p t) w -> p t w", t=PACK)
+        out_words = words_view(out_1)
+        out_codes = keep.tile([P, U], U32, align_bytes=64)
+        out_scales = keep.tile([P, U], U8, align_bytes=64)
+        out_chunks = [(0, 512), (512, 768), (768, 1024)]
+        for a, b in out_chunks:
+            last = b == U
+            res = keep.tile([P, PACK, b - a], F32, name=f"res{a}")
+            for t in range(PACK):
+                nc.vector.tensor_tensor(res[:, t, :], minus_half[t][:].indirect(n4_t[:, a // GROUP : b // GROUP]), pg[t][:, a:b], ADD)
+                if last:
+                    nc.sync.dma_start(out=out_rows[:, t, a:b], in_=res[:, t, :])
+            if not last:
+                nc.sync.dma_start(out=out_rows[:, :, a:b], in_=res[:])
+            grouped = keep.tile([P, b - a, PACK], BF16, name=f"grouped{a}", align_bytes=64)
+            dst = grouped[:].rearrange("p (c i) t -> p c t i", i=4)
+            src = res[:].rearrange("p t (c i) -> p c t i", i=4)
+            if last:
+                nc.vector.tensor_copy(dst, src)
+            else:
+                nc.scalar.copy(dst, src)
+            nc.vector.quantize_mx(out=out_codes[:, a:b].bitcast(FP8X4), scales=out_scales[:, a:b], in_=grouped[:].rearrange("p s t -> p (s t)"))
+            nc.sync.dma_start(out=out_words[:, a:b], in_=out_codes[:, a:b].bitcast(I32))
+        for q in range(QUADRANTS):
+            queue = nc.scalar if q % 2 else nc.sync
+            queue.dma_start(out=out_2[0, 4 * q : 4 * q + 4, :].bitcast(I32), in_=out_scales[32 * q : 32 * q + 4, :].bitcast(I32))

@@ -12,7 +12,6 @@ U32 = mybir.dt.uint32
 U16 = mybir.dt.uint16
 U8 = mybir.dt.uint8
 FP8X4 = mybir.dt.float8_e4m3fn_x4
-MULT = mybir.AluOpType.mult
 ADD = mybir.AluOpType.add
 COPY = mybir.ActivationFunctionType.Copy
 
@@ -26,9 +25,9 @@ def words_view(words):
     return words[0].rearrange("p n t -> p (n t)").bitcast(I32)
 
 
-def load_scale_rows(nc, plane, scales, first):
+def load_scale_rows(queue, plane, scales, first):
     for q in range(QUADRANTS):
-        nc.sync.dma_start(out=plane[32 * q + first : 32 * q + first + 4, :].bitcast(I32), in_=scales[0, 4 * q : 4 * q + 4, :].bitcast(I32))
+        queue.dma_start(out=plane[32 * q + first : 32 * q + first + 4, :].bitcast(I32), in_=scales[0, 4 * q : 4 * q + 4, :].bitcast(I32))
 
 
 def deal(nc, dealt, raw):
@@ -46,83 +45,90 @@ def tile_picked_twlputbpagem_none_po_kernel(tc, x_words, x_scales, w1_words, w1_
             nc.sync.dma_start(dst[:], src)
             return dst
 
+        def load_words(queue, src, name, tag):
+            dst = keep.tile([P, src.shape[2]], U32, name=name, tag=tag, align_bytes=64)
+            queue.dma_start(out=dst[:].bitcast(I32), in_=words_view(src))
+            return dst
+
         x_plane = keep.tile([P, T], U8, align_bytes=64, tag="page3")
-        w12_plane = keep.tile([P, H], U8, align_bytes=64, tag="w_plane")
-        nc.gpsimd.memset(x_plane[:].bitcast(I32), 0)
-        nc.vector.memset(w12_plane[:].bitcast(I32), 0)
+        w12_plane = keep.tile([P, H], U8, align_bytes=64, tag="w12_plane")
+        nc.vector.memset(x_plane[:].bitcast(I32), 0)
+        nc.gpsimd.memset(w12_plane[:].bitcast(I32), 0)
 
         offs_t = load_list(offs, "offs_t")
-        load_scale_rows(nc, x_plane, x_scales, 0)
+        load_scale_rows(nc.sync, x_plane, x_scales, 0)
+        x_codes = load_words(nc.sync, x_words, "x_codes", "page0")
         two_t = load_list(two, "two_t")
-        x_codes = keep.tile([P, T], U32, align_bytes=64, tag="page0")
-        nc.sync.dma_start(out=x_codes[:].bitcast(I32), in_=words_view(x_words))
-        w1_raw = keep.tile([P, H], U32, align_bytes=64, tag="w_raw")
-        nc.sync.dma_start(out=w1_raw[:].bitcast(I32), in_=words_view(w1_words))
-        load_scale_rows(nc, w12_plane, w1_scales, 0)
-        load_scale_rows(nc, w12_plane, w2_scales, 4)
-        w2_raw = keep.tile([P, H], U32, align_bytes=64, tag="page1")
-        nc.sync.dma_start(out=w2_raw[:].bitcast(I32), in_=words_view(w2_words))
+        w1_raw = load_words(nc.sync, w1_words, "w1_raw", "w_raw")
+        load_scale_rows(nc.sync, w12_plane, w1_scales, 0)
+        load_scale_rows(nc.sync, w12_plane, w2_scales, 4)
+        w2_raw = load_words(nc.sync, w2_words, "w2_raw", "page1")
         n1_t = load_list(n1, "n1_t")
         n2_t = load_list(n2, "n2_t")
-        gain = keep.tile([P, PACK], F32)
-        nc.sync.dma_start(out=gain[:], in_=gn.rearrange("(p t) o -> p (t o)", t=PACK))
         n3_t = load_list(n3, "n3_t")
         n4_t = load_list(n4, "n4_t")
 
         xy_scales = keep.tile([P, S], U8, align_bytes=64)
         xd_scales = keep.tile([P, S], U8, align_bytes=64, tag="page2")
-        xy_codes = keep.tile([P, S], U32, align_bytes=64)
-        xd_codes = keep.tile([P, S], U32, align_bytes=64)
-        w1_codes = keep.tile([P, H], U32, align_bytes=64)
+        xy_codes = keep.tile([P, S], U32, align_bytes=64, tag="w3_plane")
+        w1_codes = keep.tile([P, H], U32, align_bytes=64, tag="gain")
         w2_codes = keep.tile([P, H], U32, align_bytes=64)
         w12_scales = keep.tile([P, H], U8, align_bytes=64)
         nc.vector.tensor_copy(xy_scales[:], x_plane[:].indirect(offs_t[:]))
-        nc.vector.tensor_copy(xd_scales[:], x_plane[:].indirect(two_t[:]))
         nc.vector.tensor_copy(xy_codes[:], x_codes[:].indirect(offs_t[:]))
         deal(nc, w1_codes, w1_raw)
         deal(nc, w12_scales, w12_plane)
+        nc.vector.tensor_copy(xd_scales[:], x_plane[:].indirect(two_t[:]))
         deal(nc, w2_codes, w2_raw)
+        xd_codes = keep.tile([P, S], U32, align_bytes=64, tag="w12_plane")
         nc.vector.tensor_copy(xd_codes[:], x_codes[:].indirect(two_t[:]))
+
+        ys = [keep.tile([P, S], F32, name=f"minus_half_y{t}") for t in range(PACK)]
+        dd = [keep.tile([P, S], F32, name=f"d{t}") for t in range(PACK)]
+        ds = [keep.tile([P, S], F32, name=f"ds{t}") for t in range(PACK)]
 
         def product(bank, width, w_codes, w_scales, t, codes, scales, at=0):
             cols = slice(P * t, P * (t + 1))
             nc.tensor.matmul_mx(out=bank[:, at : at + width], lhsT=w_codes[:, cols].bitcast(FP8X4), lhsT_scale=w_scales[:, cols],
                                 rhs=codes.bitcast(FP8X4), rhs_scale=scales, start=True, stop=True)
 
-        ys = [keep.tile([P, S], F32, name=f"y{t}") for t in range(PACK)]
-        dd = [keep.tile([P, S], F32, name=f"d{t}") for t in range(PACK)]
+        y_banks = [psum.tile([P, S], F32, tag=f"bank{t}", name=f"ybank{t}") for t in range(PACK)]
+        d_banks = [psum.tile([P, S], F32, tag=f"bank{PACK + t}", name=f"dbank{t}") for t in range(PACK)]
         for t in range(PACK):
-            bank = psum.tile([P, S], F32, tag=f"bank{t}", name=f"ybank{t}")
-            product(bank, S, w1_codes, w12_scales[:], t, xy_codes[:], xy_scales[:])
-            nc.scalar.activation(ys[t][:], bank[:], COPY)
+            product(y_banks[t], S, w1_codes, w12_scales[:], t, xy_codes[:], xy_scales[:])
+            nc.scalar.activation(ys[t][:], y_banks[t][:], COPY, scale=-0.5)
         for t in range(PACK):
-            bank = psum.tile([P, S], F32, tag=f"bank{PACK + t}", name=f"dbank{t}")
-            product(bank, S, w2_codes, w12_scales[4:P, :], t, xd_codes[:], xd_scales[:])
-            nc.scalar.activation(dd[t][:], bank[:], COPY)
+            product(d_banks[t], S, w2_codes, w12_scales[4:P, :], t, xd_codes[:], xd_scales[:])
+            nc.scalar.activation(dd[t][:], d_banks[t][:], COPY)
+            if t > 0:
+                nc.scalar.activation(ds[t - 1][:], y_banks[t - 1][:], COPY)
+        nc.scalar.activation(ds[PACK - 1][:], y_banks[PACK - 1][:], COPY)
 
-        w3_raw = keep.tile([P, N], U32, align_bytes=64, tag="w_raw")
-        nc.sync.dma_start(out=w3_raw[:].bitcast(I32), in_=words_view(w3_words))
-        w3_plane = keep.tile([P, N], U8, align_bytes=64, tag="w_plane")
+        gain = keep.tile([P, PACK], F32, tag="gain", align_bytes=64)
+        nc.sync.dma_start(out=gain[:], in_=gn.rearrange("(p t) o -> p (t o)", t=PACK))
+        w3_raw = load_words(nc.sync, w3_words, "w3_raw", "w_raw")
+        w3_plane = keep.tile([P, N], U8, align_bytes=64, tag="w3_plane")
         nc.gpsimd.memset(w3_plane[:].bitcast(I32), 0)
-        load_scale_rows(nc, w3_plane, w3_scales, 0)
+        load_scale_rows(nc.sync, w3_plane, w3_scales, 0)
         mem_rows = mem.rearrange("(p t) w -> p t w", t=PACK)
         pg = [keep.tile([P, U], F32, name=f"pg{t}", tag=f"page{t}", align_bytes=64) for t in range(PACK)]
         for t in range(PACK):
             nc.sync.dma_start(out=pg[t][:], in_=mem_rows[:, t, :])
 
-        half_y = [keep.tile([P, W], F32, name=f"half_y{t}") for t in range(PACK - 1)]
-        half_y.append(keep.tile([P, W], F32, name="half_y3", tag="late_words", align_bytes=64))
+        picked_y = [keep.tile([P, W], F32, name=f"picked_y{t}") for t in range(PACK - 1)]
+        picked_y.append(keep.tile([P, W], F32, name="picked_y3", tag="late_words", align_bytes=64))
         picked_d = [keep.tile([P, W], F32, name=f"picked_d{t}") for t in range(PACK - 1)]
         picked_d.append(keep.tile([P, W], F32, name="picked_d3", tag="late_bytes", align_bytes=64))
         for t in range(PACK):
-            nc.vector.tensor_scalar(half_y[t][:], ys[t][:].indirect(n1_t[:]), -0.5, 0.0, MULT, ADD)
+            nc.vector.tensor_copy(picked_y[t][:], ys[t][:].indirect(n1_t[:]))
+        for t in range(PACK):
+            nc.vector.tensor_copy(picked_d[t][:], dd[t][:].indirect(n2_t[:]))
         z = keep.tile([P, S, PACK], BF16, align_bytes=64)
         z_chunks = [(0, 128), (128, 256), (256, 512)]
         for t in range(PACK):
-            nc.vector.tensor_copy(picked_d[t][:], dd[t][:].indirect(n2_t[:]))
-            nc.vector.tensor_tensor(ys[t][:].indirect(n1_t[:]), picked_d[t][:], half_y[t][:], ADD)
+            nc.vector.tensor_tensor(ds[t][:].indirect(n1_t[:]), picked_d[t][:], picked_y[t][:], ADD)
             if t < PACK - 1:
-                nc.scalar.activation(z[:, :, t], ys[t][:], COPY, scale=gain[:, t : t + 1])
+                nc.scalar.activation(z[:, :, t], ds[t][:], COPY, scale=gain[:, t : t + 1])
 
         w3_codes = keep.tile([P, N], U32, tag="late_words", align_bytes=64)
         w3_dealt = keep.tile([P, N], U8, tag="late_bytes", align_bytes=64)
@@ -135,7 +141,7 @@ def tile_picked_twlputbpagem_none_po_kernel(tc, x_words, x_scales, w1_words, w1_
 
         def quantize_z(a, b):
             t = PACK - 1
-            nc.scalar.activation(z[:, a:b, t], ys[t][:, a:b], COPY, scale=gain[:, t : t + 1])
+            nc.scalar.activation(z[:, a:b, t], ds[t][:, a:b], COPY, scale=gain[:, t : t + 1])
             nc.vector.quantize_mx(out=z_codes[:, a:b].bitcast(FP8X4), scales=z_scales[:, a:b], in_=z[:, a:b, :].rearrange("p s t -> p (s t)"))
 
         def scatter_h(t, a, b):
@@ -163,31 +169,38 @@ def tile_picked_twlputbpagem_none_po_kernel(tc, x_words, x_scales, w1_words, w1_
                 first = 0
             nc.scalar.activation(hs[t][:, first:S], bank[:, first:S], COPY)
             scatter_h(t, first, S)
+        for t in range(PACK):
             nc.scalar.activation(minus_half[t][:], pg[t][:], COPY, scale=-0.5)
 
         out_rows = out_0.rearrange("(p t) w -> p t w", t=PACK)
         out_words = words_view(out_1)
         out_codes = keep.tile([P, U], U32, align_bytes=64)
         out_scales = keep.tile([P, U], U8, align_bytes=64)
-        out_chunks = [(0, 512), (512, 768), (768, 1024)]
-        for a, b in out_chunks:
-            last = b == U
-            res = keep.tile([P, PACK, b - a], F32, name=f"res{a}")
+        width = 256
+        chunks = U // width
+
+        def round_and_quantize(copy, res, a, lo, hi, tag):
+            grouped = keep.tile([P, hi - lo, PACK], BF16, name=f"grouped{a + lo}", tag=tag, align_bytes=64)
+            copy(grouped[:].rearrange("p (c i) t -> p c t i", i=4), res[:, :, lo:hi].rearrange("p t (c i) -> p c t i", i=4))
+            cols = slice(a + lo, a + hi)
+            nc.vector.quantize_mx(out=out_codes[:, cols].bitcast(FP8X4), scales=out_scales[:, cols], in_=grouped[:].rearrange("p s t -> p (s t)"))
+
+        for c in range(chunks):
+            a, b = c * width, (c + 1) * width
+            last = c == chunks - 1
+            res = keep.tile([P, PACK, width], F32, name=f"res{c}", tag=f"slot{c}", align_bytes=64)
             for t in range(PACK):
                 nc.vector.tensor_tensor(res[:, t, :], minus_half[t][:].indirect(n4_t[:, a // GROUP : b // GROUP]), pg[t][:, a:b], ADD)
-                if last:
-                    nc.sync.dma_start(out=out_rows[:, t, a:b], in_=res[:, t, :])
-            if not last:
-                nc.sync.dma_start(out=out_rows[:, :, a:b], in_=res[:])
-            grouped = keep.tile([P, b - a, PACK], BF16, name=f"grouped{a}", align_bytes=64)
-            dst = grouped[:].rearrange("p (c i) t -> p c t i", i=4)
-            src = res[:].rearrange("p t (c i) -> p c t i", i=4)
+                if last and t == PACK - 2:
+                    nc.sync.dma_start(out=out_rows[:, 0 : t + 1, a:b], in_=res[:, 0 : t + 1, :])
             if last:
-                nc.vector.tensor_copy(dst, src)
+                nc.sync.dma_start(out=out_rows[:, PACK - 1, a:b], in_=res[:, PACK - 1, :])
+                round_and_quantize(nc.vector.tensor_copy, res, a, 0, width // 2, f"slot{chunks}")
+                round_and_quantize(nc.scalar.copy, res, a, width // 2, width, f"slot{chunks + 1}")
             else:
-                nc.scalar.copy(dst, src)
-            nc.vector.quantize_mx(out=out_codes[:, a:b].bitcast(FP8X4), scales=out_scales[:, a:b], in_=grouped[:].rearrange("p s t -> p (s t)"))
+                nc.sync.dma_start(out=out_rows[:, :, a:b], in_=res[:])
+                round_and_quantize(nc.scalar.copy, res, a, 0, width, f"slot{c + 2}")
             nc.sync.dma_start(out=out_words[:, a:b], in_=out_codes[:, a:b].bitcast(I32))
         for q in range(QUADRANTS):
-            queue = nc.scalar if q % 2 else nc.sync
+            queue = nc.sync if q % 2 else nc.scalar
             queue.dma_start(out=out_2[0, 4 * q : 4 * q + 4, :].bitcast(I32), in_=out_scales[32 * q : 32 * q + 4, :].bitcast(I32))

@@ -34,6 +34,10 @@ def deal(nc, dealt, raw):
     nc.vector.tensor_copy(out=dealt[:].rearrange("p (t m) -> p m t", t=PACK), in_=raw[:].rearrange("p (m t) -> p m t", t=PACK))
 
 
+def deal_bytes(nc, dealt, raw):
+    nc.vector.tensor_copy(out=dealt[:].rearrange("p (t m) -> p t m", t=PACK), in_=raw[:].rearrange("p (m t) -> p t m", t=PACK))
+
+
 def tile_picked_twlputbpagem_none_po_kernel(tc, x_words, x_scales, w1_words, w1_scales, w2_words, w2_scales, gn, w3_words, w3_scales, mem, offs, two, n1, n2, n3, n4, out_0, out_1, out_2):
     nc = tc.nc
     with ExitStack() as ctx:
@@ -50,34 +54,36 @@ def tile_picked_twlputbpagem_none_po_kernel(tc, x_words, x_scales, w1_words, w1_
             queue.dma_start(out=dst[:].bitcast(I32), in_=words_view(src))
             return dst
 
-        x_plane = keep.tile([P, T], U8, align_bytes=64, tag="page3")
+        x_plane = keep.tile([P, T], U8, align_bytes=64)
         w12_plane = keep.tile([P, H], U8, align_bytes=64, tag="w12_plane")
+        w3_plane = keep.tile([P, N], U8, align_bytes=64)
         nc.vector.memset(x_plane[:].bitcast(I32), 0)
         nc.gpsimd.memset(w12_plane[:].bitcast(I32), 0)
+        nc.gpsimd.memset(w3_plane[:].bitcast(I32), 0)
 
         offs_t = load_list(offs, "offs_t")
         load_scale_rows(nc.sync, x_plane, x_scales, 0)
-        x_codes = load_words(nc.sync, x_words, "x_codes", "page0")
+        x_codes = load_words(nc.sync, x_words, "x_codes", "x_codes")
         two_t = load_list(two, "two_t")
-        w1_raw = load_words(nc.sync, w1_words, "w1_raw", "w_raw")
+        w1_raw = load_words(nc.sync, w1_words, "w1_raw", "w1_raw")
         load_scale_rows(nc.sync, w12_plane, w1_scales, 0)
         load_scale_rows(nc.sync, w12_plane, w2_scales, 4)
-        w2_raw = load_words(nc.sync, w2_words, "w2_raw", "page1")
+        w2_raw = load_words(nc.sync, w2_words, "w2_raw", "w2_raw")
         n1_t = load_list(n1, "n1_t")
         n2_t = load_list(n2, "n2_t")
         n3_t = load_list(n3, "n3_t")
         n4_t = load_list(n4, "n4_t")
 
         xy_scales = keep.tile([P, S], U8, align_bytes=64)
-        xd_scales = keep.tile([P, S], U8, align_bytes=64, tag="page2")
-        xy_codes = keep.tile([P, S], U32, align_bytes=64, tag="w3_plane")
-        w1_codes = keep.tile([P, H], U32, align_bytes=64, tag="gain")
+        xd_scales = keep.tile([P, S], U8, align_bytes=64)
+        xy_codes = keep.tile([P, S], U32, align_bytes=64)
+        w1_codes = keep.tile([P, H], U32, align_bytes=64)
         w2_codes = keep.tile([P, H], U32, align_bytes=64)
         w12_scales = keep.tile([P, H], U8, align_bytes=64)
         nc.vector.tensor_copy(xy_scales[:], x_plane[:].indirect(offs_t[:]))
         nc.vector.tensor_copy(xy_codes[:], x_codes[:].indirect(offs_t[:]))
         deal(nc, w1_codes, w1_raw)
-        deal(nc, w12_scales, w12_plane)
+        deal_bytes(nc, w12_scales, w12_plane)
         nc.vector.tensor_copy(xd_scales[:], x_plane[:].indirect(two_t[:]))
         deal(nc, w2_codes, w2_raw)
         xd_codes = keep.tile([P, S], U32, align_bytes=64, tag="w12_plane")
@@ -104,14 +110,12 @@ def tile_picked_twlputbpagem_none_po_kernel(tc, x_words, x_scales, w1_words, w1_
                 nc.scalar.activation(ds[t - 1][:], y_banks[t - 1][:], COPY)
         nc.scalar.activation(ds[PACK - 1][:], y_banks[PACK - 1][:], COPY)
 
-        gain = keep.tile([P, PACK], F32, tag="gain", align_bytes=64)
+        gain = keep.tile([P, PACK], F32)
         nc.sync.dma_start(out=gain[:], in_=gn.rearrange("(p t) o -> p (t o)", t=PACK))
-        w3_raw = load_words(nc.sync, w3_words, "w3_raw", "w_raw")
-        w3_plane = keep.tile([P, N], U8, align_bytes=64, tag="w3_plane")
-        nc.gpsimd.memset(w3_plane[:].bitcast(I32), 0)
+        w3_raw = load_words(nc.sync, w3_words, "w3_raw", "w3_raw")
         load_scale_rows(nc.sync, w3_plane, w3_scales, 0)
         mem_rows = mem.rearrange("(p t) w -> p t w", t=PACK)
-        pg = [keep.tile([P, U], F32, name=f"pg{t}", tag=f"page{t}", align_bytes=64) for t in range(PACK)]
+        pg = [keep.tile([P, U], F32, name=f"pg{t}") for t in range(PACK)]
         for t in range(PACK):
             nc.sync.dma_start(out=pg[t][:], in_=mem_rows[:, t, :])
 
@@ -133,7 +137,7 @@ def tile_picked_twlputbpagem_none_po_kernel(tc, x_words, x_scales, w1_words, w1_
         w3_codes = keep.tile([P, N], U32, tag="late_words", align_bytes=64)
         w3_dealt = keep.tile([P, N], U8, tag="late_bytes", align_bytes=64)
         deal(nc, w3_codes, w3_raw)
-        deal(nc, w3_dealt, w3_plane)
+        deal_bytes(nc, w3_dealt, w3_plane)
 
         z_codes = keep.tile([P, S], U32, align_bytes=64)
         z_scales = keep.tile([P, S], U8, align_bytes=64)

@@ -25,8 +25,8 @@ def words_view(words):
     return words[0].rearrange("p n t -> p (n t)").bitcast(I32)
 
 
-def load_scale_rows(queue, plane, scales, first):
-    for q in range(QUADRANTS):
+def load_scale_rows(queue, plane, scales, first, quadrants=range(QUADRANTS)):
+    for q in quadrants:
         queue.dma_start(out=plane[32 * q + first : 32 * q + first + 4, :].bitcast(I32), in_=scales[0, 4 * q : 4 * q + 4, :].bitcast(I32))
 
 
@@ -63,10 +63,11 @@ def tile_picked_twlputbpagem_none_po_kernel(tc, x_words, x_scales, w1_words, w1_
 
         offs_t = load_list(offs, "offs_t")
         load_scale_rows(nc.sync, x_plane, x_scales, 0)
-        x_codes = load_words(nc.sync, x_words, "x_codes", "x_codes")
-        two_t = load_list(two, "two_t")
         w1_raw = load_words(nc.sync, w1_words, "w1_raw", "w1_raw")
-        load_scale_rows(nc.sync, w12_plane, w1_scales, 0)
+        two_t = load_list(two, "two_t")
+        load_scale_rows(nc.gpsimd, w12_plane, w1_scales, 0, range(1))
+        x_codes = load_words(nc.sync, x_words, "x_codes", "x_codes")
+        load_scale_rows(nc.sync, w12_plane, w1_scales, 0, range(1, QUADRANTS))
         load_scale_rows(nc.sync, w12_plane, w2_scales, 4)
         w2_raw = load_words(nc.sync, w2_words, "w2_raw", "w2_raw")
         n1_t = load_list(n1, "n1_t")
@@ -74,17 +75,17 @@ def tile_picked_twlputbpagem_none_po_kernel(tc, x_words, x_scales, w1_words, w1_
         n3_t = load_list(n3, "n3_t")
         n4_t = load_list(n4, "n4_t")
 
-        xy_scales = keep.tile([P, S], U8, align_bytes=64)
         xd_scales = keep.tile([P, S], U8, align_bytes=64)
         xy_codes = keep.tile([P, S], U32, align_bytes=64)
         w1_codes = keep.tile([P, H], U32, align_bytes=64)
         w2_codes = keep.tile([P, H], U32, align_bytes=64)
         w12_scales = keep.tile([P, H], U8, align_bytes=64)
-        nc.vector.tensor_copy(xy_scales[:], x_plane[:].indirect(offs_t[:]))
-        nc.vector.tensor_copy(xy_codes[:], x_codes[:].indirect(offs_t[:]))
         deal(nc, w1_codes, w1_raw)
-        deal_bytes(nc, w12_scales, w12_plane)
+        xy_scales = keep.tile([P, S], U8, align_bytes=64, tag="w1_raw")
+        nc.vector.tensor_copy(xy_scales[:], x_plane[:].indirect(offs_t[:]))
         nc.vector.tensor_copy(xd_scales[:], x_plane[:].indirect(two_t[:]))
+        nc.vector.tensor_copy(xy_codes[:], x_codes[:].indirect(offs_t[:]))
+        deal_bytes(nc, w12_scales, w12_plane)
         deal(nc, w2_codes, w2_raw)
         xd_codes = keep.tile([P, S], U32, align_bytes=64, tag="w12_plane")
         nc.vector.tensor_copy(xd_codes[:], x_codes[:].indirect(two_t[:]))

@@ -14,6 +14,7 @@ U8 = mybir.dt.uint8
 FP8X4 = mybir.dt.float8_e4m3fn_x4
 ADD = mybir.AluOpType.add
 COPY = mybir.ActivationFunctionType.Copy
+IDENTITY = mybir.ActivationFunctionType.Identity
 
 P = 128
 PACK = 4
@@ -174,8 +175,12 @@ def tile_picked_twlputbpagem_none_po_kernel(tc, x_words, x_scales, w1_words, w1_
                 first = 0
             nc.scalar.activation(hs[t][:, first:S], bank[:, first:S], COPY)
             scatter_h(t, first, S)
+        scale = keep.tile([P, 1], F32, tag="scale", align_bytes=64)
+        bias = keep.tile([P, 1], F32, tag="bias", align_bytes=64)
+        nc.vector.memset(scale[:], -0.5)
+        nc.vector.memset(bias[:], 0.0)
         for t in range(PACK):
-            nc.scalar.activation(minus_half[t][:], pg[t][:], COPY, scale=-0.5)
+            nc.scalar.activation(minus_half[t][:], pg[t][:], IDENTITY, bias=bias[:], scale=scale[:])
 
         out_rows = out_0.rearrange("(p t) w -> p t w", t=PACK)
         out_words = words_view(out_1)
@@ -183,9 +188,10 @@ def tile_picked_twlputbpagem_none_po_kernel(tc, x_words, x_scales, w1_words, w1_
         out_scales = keep.tile([P, U], U8, align_bytes=64)
         width = 256
         chunks = U // width
+        res_tags = ["res0", "scale", "bias", "grouped0"]
 
-        def round_and_quantize(copy, res, a, lo, hi, tag):
-            grouped = keep.tile([P, hi - lo, PACK], BF16, name=f"grouped{a + lo}", tag=tag, align_bytes=64)
+        def round_and_quantize(copy, res, a, lo, hi):
+            grouped = keep.tile([P, hi - lo, PACK], BF16, name=f"grouped{a + lo}", tag=f"grouped{a + lo}", align_bytes=64)
             copy(grouped[:].rearrange("p (c i) t -> p c t i", i=4), res[:, :, lo:hi].rearrange("p t (c i) -> p c t i", i=4))
             cols = slice(a + lo, a + hi)
             nc.vector.quantize_mx(out=out_codes[:, cols].bitcast(FP8X4), scales=out_scales[:, cols], in_=grouped[:].rearrange("p s t -> p (s t)"))
@@ -193,18 +199,18 @@ def tile_picked_twlputbpagem_none_po_kernel(tc, x_words, x_scales, w1_words, w1_
         for c in range(chunks):
             a, b = c * width, (c + 1) * width
             last = c == chunks - 1
-            res = keep.tile([P, PACK, width], F32, name=f"res{c}", tag=f"slot{c}", align_bytes=64)
+            res = keep.tile([P, PACK, width], F32, name=f"res{c}", tag=res_tags[c], align_bytes=64)
             for t in range(PACK):
                 nc.vector.tensor_tensor(res[:, t, :], minus_half[t][:].indirect(n4_t[:, a // GROUP : b // GROUP]), pg[t][:, a:b], ADD)
                 if last and t == PACK - 2:
                     nc.sync.dma_start(out=out_rows[:, 0 : t + 1, a:b], in_=res[:, 0 : t + 1, :])
             if last:
                 nc.sync.dma_start(out=out_rows[:, PACK - 1, a:b], in_=res[:, PACK - 1, :])
-                round_and_quantize(nc.vector.tensor_copy, res, a, 0, width // 2, f"slot{chunks}")
-                round_and_quantize(nc.scalar.copy, res, a, width // 2, width, f"slot{chunks + 1}")
+                round_and_quantize(nc.vector.tensor_copy, res, a, 0, width // 2)
+                round_and_quantize(nc.scalar.copy, res, a, width // 2, width)
             else:
                 nc.sync.dma_start(out=out_rows[:, :, a:b], in_=res[:])
-                round_and_quantize(nc.scalar.copy, res, a, 0, width, f"slot{c + 2}")
+                round_and_quantize(nc.scalar.copy, res, a, 0, width)
             nc.sync.dma_start(out=out_words[:, a:b], in_=out_codes[:, a:b].bitcast(I32))
         for q in range(QUADRANTS):
             queue = nc.sync if q % 2 else nc.scalar

from contextlib import ExitStack

import concourse.mybir as mybir

K, T, S, N, H, W, U = 512, 2048, 512, 512, 512, 256, 1024
FLOPS = 2 * K * H * S * 2 + 2 * H * N * S

F32 = mybir.dt.float32
BF16 = mybir.dt.bfloat16
I32 = mybir.dt.int32
U32 = mybir.dt.uint32
U16 = mybir.dt.uint16
U8 = mybir.dt.uint8
FP8X4 = mybir.dt.float8_e4m3fn_x4
ADD = mybir.AluOpType.add
COPY = mybir.ActivationFunctionType.Copy
IDENTITY = mybir.ActivationFunctionType.Identity

P = 128
PACK = 4
QUADRANTS = 4
GROUP = 16


def words_view(words):
    return words[0].rearrange("p n t -> p (n t)").bitcast(I32)


def load_scale_rows(queue, plane, scales, first, quadrants=range(QUADRANTS)):
    for q in quadrants:
        queue.dma_start(out=plane[32 * q + first : 32 * q + first + 4, :].bitcast(I32), in_=scales[0, 4 * q : 4 * q + 4, :].bitcast(I32))


def deal(nc, dealt, raw):
    nc.vector.tensor_copy(out=dealt[:].rearrange("p (t m) -> p m t", t=PACK), in_=raw[:].rearrange("p (m t) -> p m t", t=PACK))


def deal_bytes(nc, dealt, raw):
    nc.vector.tensor_copy(out=dealt[:].rearrange("p (t m) -> p t m", t=PACK), in_=raw[:].rearrange("p (m t) -> p t m", t=PACK))


def tile_picked_twlputbpagem_none_po_kernel(tc, x_words, x_scales, w1_words, w1_scales, w2_words, w2_scales, gn, w3_words, w3_scales, mem, offs, two, n1, n2, n3, n4, out_0, out_1, out_2):
    nc = tc.nc
    with ExitStack() as ctx:
        keep = ctx.enter_context(tc.tile_pool(name="keep", bufs=1))
        psum = ctx.enter_context(tc.psum_pool(name="psum", bufs=1))

        def load_list(src, name):
            dst = keep.tile(list(src.shape), U16, name=name)
            nc.sync.dma_start(dst[:], src)
            return dst

        def load_words(queue, src, name, tag):
            dst = keep.tile([P, src.shape[2]], U32, name=name, tag=tag, align_bytes=64)
            queue.dma_start(out=dst[:].bitcast(I32), in_=words_view(src))
            return dst

        x_plane = keep.tile([P, T], U8, align_bytes=64)
        w12_plane = keep.tile([P, H], U8, align_bytes=64, tag="w12_plane")
        w3_plane = keep.tile([P, N], U8, align_bytes=64)
        nc.vector.memset(x_plane[:].bitcast(I32), 0)
        nc.gpsimd.memset(w12_plane[:].bitcast(I32), 0)
        nc.gpsimd.memset(w3_plane[:].bitcast(I32), 0)

        offs_t = load_list(offs, "offs_t")
        load_scale_rows(nc.sync, x_plane, x_scales, 0)
        w1_raw = load_words(nc.sync, w1_words, "w1_raw", "w1_raw")
        two_t = load_list(two, "two_t")
        load_scale_rows(nc.gpsimd, w12_plane, w1_scales, 0, range(1))
        x_codes = load_words(nc.sync, x_words, "x_codes", "x_codes")
        load_scale_rows(nc.sync, w12_plane, w1_scales, 0, range(1, QUADRANTS))
        load_scale_rows(nc.sync, w12_plane, w2_scales, 4)
        w2_raw = load_words(nc.sync, w2_words, "w2_raw", "w2_raw")
        n1_t = load_list(n1, "n1_t")
        n2_t = load_list(n2, "n2_t")
        n3_t = load_list(n3, "n3_t")
        n4_t = load_list(n4, "n4_t")

        xd_scales = keep.tile([P, S], U8, align_bytes=64)
        xy_codes = keep.tile([P, S], U32, align_bytes=64)
        w1_codes = keep.tile([P, H], U32, align_bytes=64)
        w2_codes = keep.tile([P, H], U32, align_bytes=64)
        w12_scales = keep.tile([P, H], U8, align_bytes=64)
        deal(nc, w1_codes, w1_raw)
        xy_scales = keep.tile([P, S], U8, align_bytes=64, tag="w1_raw")
        nc.vector.tensor_copy(xy_scales[:], x_plane[:].indirect(offs_t[:]))
        nc.vector.tensor_copy(xd_scales[:], x_plane[:].indirect(two_t[:]))
        nc.vector.tensor_copy(xy_codes[:], x_codes[:].indirect(offs_t[:]))
        deal_bytes(nc, w12_scales, w12_plane)
        deal(nc, w2_codes, w2_raw)
        xd_codes = keep.tile([P, S], U32, align_bytes=64, tag="w12_plane")
        nc.vector.tensor_copy(xd_codes[:], x_codes[:].indirect(two_t[:]))

        ys = [keep.tile([P, S], F32, name=f"minus_half_y{t}") for t in range(PACK)]
        dd = [keep.tile([P, S], F32, name=f"d{t}") for t in range(PACK)]
        ds = [keep.tile([P, S], F32, name=f"ds{t}") for t in range(PACK)]

        def product(bank, width, w_codes, w_scales, t, codes, scales, at=0):
            cols = slice(P * t, P * (t + 1))
            nc.tensor.matmul_mx(out=bank[:, at : at + width], lhsT=w_codes[:, cols].bitcast(FP8X4), lhsT_scale=w_scales[:, cols],
                                rhs=codes.bitcast(FP8X4), rhs_scale=scales, start=True, stop=True)

        y_banks = [psum.tile([P, S], F32, tag=f"bank{t}", name=f"ybank{t}") for t in range(PACK)]
        d_banks = [psum.tile([P, S], F32, tag=f"bank{PACK + t}", name=f"dbank{t}") for t in range(PACK)]
        for t in range(PACK):
            product(y_banks[t], S, w1_codes, w12_scales[:], t, xy_codes[:], xy_scales[:])
            nc.scalar.activation(ys[t][:], y_banks[t][:], COPY, scale=-0.5)
        for t in range(PACK):
            product(d_banks[t], S, w2_codes, w12_scales[4:P, :], t, xd_codes[:], xd_scales[:])
            nc.scalar.activation(dd[t][:], d_banks[t][:], COPY)
            if t > 0:
                nc.scalar.activation(ds[t - 1][:], y_banks[t - 1][:], COPY)
        nc.scalar.activation(ds[PACK - 1][:], y_banks[PACK - 1][:], COPY)

        gain = keep.tile([P, PACK], F32)
        nc.sync.dma_start(out=gain[:], in_=gn.rearrange("(p t) o -> p (t o)", t=PACK))
        w3_raw = load_words(nc.sync, w3_words, "w3_raw", "w3_raw")
        load_scale_rows(nc.sync, w3_plane, w3_scales, 0)
        mem_rows = mem.rearrange("(p t) w -> p t w", t=PACK)
        pg = [keep.tile([P, U], F32, name=f"pg{t}") for t in range(PACK)]
        for t in range(PACK):
            nc.sync.dma_start(out=pg[t][:], in_=mem_rows[:, t, :])

        picked_y = [keep.tile([P, W], F32, name=f"picked_y{t}") for t in range(PACK - 1)]
        picked_y.append(keep.tile([P, W], F32, name="picked_y3", tag="late_words", align_bytes=64))
        picked_d = [keep.tile([P, W], F32, name=f"picked_d{t}") for t in range(PACK - 1)]
        picked_d.append(keep.tile([P, W], F32, name="picked_d3", tag="late_bytes", align_bytes=64))
        for t in range(PACK):
            nc.vector.tensor_copy(picked_y[t][:], ys[t][:].indirect(n1_t[:]))
        for t in range(PACK):
            nc.vector.tensor_copy(picked_d[t][:], dd[t][:].indirect(n2_t[:]))
        z = keep.tile([P, S, PACK], BF16, align_bytes=64)
        z_chunks = [(0, 128), (128, 256), (256, 512)]
        for t in range(PACK):
            nc.vector.tensor_tensor(ds[t][:].indirect(n1_t[:]), picked_d[t][:], picked_y[t][:], ADD)
            if t < PACK - 1:
                nc.scalar.activation(z[:, :, t], ds[t][:], COPY, scale=gain[:, t : t + 1])

        w3_codes = keep.tile([P, N], U32, tag="late_words", align_bytes=64)
        w3_dealt = keep.tile([P, N], U8, tag="late_bytes", align_bytes=64)
        deal(nc, w3_codes, w3_raw)
        deal_bytes(nc, w3_dealt, w3_plane)

        z_codes = keep.tile([P, S], U32, align_bytes=64)
        z_scales = keep.tile([P, S], U8, align_bytes=64)
        hs = [keep.tile([P, S], F32, name=f"h{t}") for t in range(PACK)]

        def quantize_z(a, b):
            t = PACK - 1
            nc.scalar.activation(z[:, a:b, t], ds[t][:, a:b], COPY, scale=gain[:, t : t + 1])
            nc.vector.quantize_mx(out=z_codes[:, a:b].bitcast(FP8X4), scales=z_scales[:, a:b], in_=z[:, a:b, :].rearrange("p s t -> p (s t)"))

        def scatter_h(t, a, b):
            nc.vector.tensor_copy(pg[t][:].indirect(n3_t[:, a // GROUP : b // GROUP]), hs[t][:, a:b])

        a0, b0 = z_chunks[0]
        quantize_z(a0, b0)
        early = range(2)
        for t in early:
            bank = psum.tile([P, S], F32, tag=f"bank{t}", name=f"hbank_a{t}")
            product(bank, b0, w3_codes, w3_dealt[:], t, z_codes[:, a0:b0], z_scales[:, a0:b0])
            nc.scalar.activation(hs[t][:, a0:b0], bank[:, a0:b0], COPY)
            scatter_h(t, a0, b0)
        for a, b in z_chunks[1:]:
            quantize_z(a, b)
        minus_half = [keep.tile([P, U], F32, name=f"minus_half{t}") for t in range(PACK)]
        for t in range(PACK):
            bank = psum.tile([P, S], F32, tag=f"bank{PACK + t}", name=f"hbank_b{t}")
            if t in early:
                for a, b in z_chunks[1:]:
                    product(bank, b - a, w3_codes, w3_dealt[:], t, z_codes[:, a:b], z_scales[:, a:b], at=a)
                first = b0
            else:
                product(bank, S, w3_codes, w3_dealt[:], t, z_codes[:], z_scales[:])
                first = 0
            nc.scalar.activation(hs[t][:, first:S], bank[:, first:S], COPY)
            scatter_h(t, first, S)
        scale = keep.tile([P, 1], F32, tag="scale", align_bytes=64)
        bias = keep.tile([P, 1], F32, tag="bias", align_bytes=64)
        nc.vector.memset(scale[:], -0.5)
        nc.vector.memset(bias[:], 0.0)
        for t in range(PACK):
            nc.scalar.activation(minus_half[t][:], pg[t][:], IDENTITY, bias=bias[:], scale=scale[:])

        out_rows = out_0.rearrange("(p t) w -> p t w", t=PACK)
        out_words = words_view(out_1)
        out_codes = keep.tile([P, U], U32, align_bytes=64)
        out_scales = keep.tile([P, U], U8, align_bytes=64)
        width = 256
        chunks = U // width
        res_tags = ["res0", "scale", "bias", "grouped0"]

        def round_and_quantize(copy, res, a, lo, hi):
            grouped = keep.tile([P, hi - lo, PACK], BF16, name=f"grouped{a + lo}", tag=f"grouped{a + lo}", align_bytes=64)
            copy(grouped[:].rearrange("p (c i) t -> p c t i", i=4), res[:, :, lo:hi].rearrange("p t (c i) -> p c t i", i=4))
            cols = slice(a + lo, a + hi)
            nc.vector.quantize_mx(out=out_codes[:, cols].bitcast(FP8X4), scales=out_scales[:, cols], in_=grouped[:].rearrange("p s t -> p (s t)"))

        for c in range(chunks):
            a, b = c * width, (c + 1) * width
            last = c == chunks - 1
            res = keep.tile([P, PACK, width], F32, name=f"res{c}", tag=res_tags[c], align_bytes=64)
            for t in range(PACK):
                nc.vector.tensor_tensor(res[:, t, :], minus_half[t][:].indirect(n4_t[:, a // GROUP : b // GROUP]), pg[t][:, a:b], ADD)
                if last and t == PACK - 2:
                    nc.sync.dma_start(out=out_rows[:, 0 : t + 1, a:b], in_=res[:, 0 : t + 1, :])
            if last:
                nc.sync.dma_start(out=out_rows[:, PACK - 1, a:b], in_=res[:, PACK - 1, :])
                round_and_quantize(nc.vector.tensor_copy, res, a, 0, width // 2)
                round_and_quantize(nc.scalar.copy, res, a, width // 2, width)
            else:
                nc.sync.dma_start(out=out_rows[:, :, a:b], in_=res[:])
                round_and_quantize(nc.scalar.copy, res, a, 0, width)
            nc.sync.dma_start(out=out_words[:, a:b], in_=out_codes[:, a:b].bitcast(I32))
        for q in range(QUADRANTS):
            queue = nc.sync if q % 2 else nc.scalar
            queue.dma_start(out=out_2[0, 4 * q : 4 * q + 4, :].bitcast(I32), in_=out_scales[32 * q : 32 * q + 4, :].bitcast(I32))
